import numpy as np
import ml_dtypes


def mxq(x, axis, fmt="e4m3"):
    dtype, down = {"e4m3": (ml_dtypes.float8_e4m3fn, 7), "e5m2": (ml_dtypes.float8_e5m2, 14)}[fmt]
    v = np.moveaxis(np.asarray(x, np.float32).astype(ml_dtypes.bfloat16).astype(np.float64), axis, -1)
    blocks = v.reshape(v.shape[:-1] + (-1, 32))
    amax = np.abs(blocks).max(-1, keepdims=True)
    byte = np.maximum(np.where(amax > 0, np.frexp(amax)[1] - 1 + 127, 0) - down, 1)
    scale = np.exp2(byte - 127.0)
    codes = (blocks / scale).astype(np.float32).astype(dtype).astype(np.float64)
    return np.moveaxis((codes * scale).reshape(v.shape), -1, axis)


WIDE = False


def mx_kscale(k):
    if not WIDE:
        return np.ones(k)
    levels = np.array([10, -10, 5, -5, 0])
    if k % 512:
        return np.exp2(np.random.permutation(np.resize(levels, k // 32))).repeat(32)
    a = np.empty((k // 512, 16))
    for p in range(k // 512):
        a[p, :8] = np.random.permutation(np.resize(levels, 8))
        for g in range(8):
            far = levels[np.abs(levels - a[p, g]) >= 10]
            a[p, g + 8] = far[np.random.randint(len(far))]
    return np.exp2(a.ravel()).repeat(32)


def f64(x):
    return np.asarray(x).astype(np.float64)


def striped(idx):
    return np.tile(idx.reshape(-1, 16).T, (8, 1)).astype(np.uint16)


def unstriped(offs):
    return offs[:16].T.reshape(-1).astype(np.int64)


def striped8(idx):
    return np.concatenate([x.reshape(-1, 16).T for x in idx]).astype(np.uint16)


def runs(offs, k):
    lists = np.stack([offs[16 * r : 16 * r + 16].T.reshape(-1) for r in range(8)]).astype(np.int64)
    return lists[np.arange(k) % 512 // 64]


def pack_weight(w):
    k, n = w.shape
    w = f64(np.asarray(w, np.float32).astype(ml_dtypes.bfloat16)).reshape(k // 32, 32, n)
    amax = np.abs(w).max(1)
    byte = np.clip(np.where(amax > 0, np.frexp(amax)[1] - 1 + 127 - 7, 1), 1, 254)
    scaled = (w * np.exp2(127.0 - byte)[:, None, :]).reshape(k, n).astype(np.float32)
    words = np.ascontiguousarray(scaled.reshape(k // 512, 128, 4, n).transpose(0, 1, 3, 2)).astype(ml_dtypes.float8_e4m3fn).view(np.uint8)
    return words, np.ascontiguousarray(byte.astype(np.uint8).reshape(k // 512, 16, n))


def unpack_weight(words, scales):
    g, p, n, _ = words.shape
    vals = np.ascontiguousarray(words).view(ml_dtypes.float8_e4m3fn).astype(np.float64) * np.repeat(np.exp2(scales.astype(np.float64) - 127.0), 8, axis=1)[..., None]
    return vals.transpose(0, 1, 3, 2).reshape(g * 512, n)


def sigmoid(v):
    return 1.0 / (1.0 + np.exp(-np.maximum(v, -700.0)))


K, T, S, N, H, G, U = 512, 1024, 512, 512, 512, 2048, 1024


def setup_inputs():
    n = np.random.standard_normal
    s = mx_kscale(K)[:, None]
    u = mx_kscale(S)
    packed_xT = pack_weight(n((K, T)) * s)
    packed_dT = pack_weight(n((K, G)) / s)
    return {
        "x_words": packed_xT[0],
        "x_scales": packed_xT[1],
        "w1": (n((K, H)) / np.sqrt(K) / s).astype(np.float32),
        "gs": (np.random.uniform(0.5, 1.5, (K, 1)) * s).astype(np.float32),
        "d_words": packed_dT[0],
        "d_scales": packed_dT[1],
        "mem": n((H, U)).astype(np.float32),
        "res": (1.5 * n((N, U))).astype(np.float32),
        "gn": (np.random.uniform(0.5, 1.5, (H, 1)) * u[:, None]).astype(np.float32),
        "w2": (n((H, N)) / np.sqrt(H) / u[:, None]).astype(np.float32),
        "offs": striped(np.random.permutation(T)[:S]),
        "n1": striped8(np.stack([np.random.permutation(S) for _ in range(8)])),
        "n2": striped8(np.stack([np.random.permutation(S) for _ in range(8)])),
        "kidx": striped8(np.random.randint(0, G, (8, H))),
        "n3": striped8(np.stack([np.random.permutation(U)[:S] for _ in range(8)])),
    }


def reference(x_words, x_scales, w1, gs, d_words, d_scales, mem, res, gn, w2, offs, n1, n2, kidx, n3):
    d_kidx = unpack_weight(d_words, d_scales)[np.arange(K)[:, None], runs(kidx, K)]
    xq = unpack_weight(x_words, x_scales)[:, unstriped(offs)]
    y = mxq(f64(w1), 0, "e4m3").T @ xq
    z = f64(gs) * (y + (sigmoid(y[np.arange(H)[:, None], runs(n1, H)])) * (y[np.arange(H)[:, None], runs(n2, H)] - y))
    s = 0.0625 * ((d_kidx.T @ mxq(z, 0, "e4m3")))
    nw = np.maximum(s, 0.5 * (f64(mem)[np.arange(H)[:, None], runs(n3, H)]))
    pg = f64(mem).copy()
    pg[np.arange(H)[:, None], runs(n3, H)] = nw
    z2 = f64(gn) * pg
    return f64(res) + (mxq(f64(w2), 0, "e4m3").T @ mxq(z2, 0, "e4m3"))

@@ -1,0 +1,202 @@
+from contextlib import ExitStack
+
+import concourse.mybir as mybir
+
+K, T, S, N, H, G, U = 512, 1024, 512, 512, 512, 2048, 1024
+FLOPS = 2 * K * H * S + 2 * K * H * S + 2 * H * N * U
+
+F32 = mybir.dt.float32
+BF16 = mybir.dt.bfloat16
+I32 = mybir.dt.int32
+U32 = mybir.dt.uint32
+U16 = mybir.dt.uint16
+U8 = mybir.dt.uint8
+FP8X4 = mybir.dt.float8_e4m3fn_x4
+ALU = mybir.AluOpType
+ACT = mybir.ActivationFunctionType
+
+P = 128
+PACK = 4
+CHUNK = 256
+
+
+def tile_picked_pqktrackpagex_none_p_kernel(
+    tc, x_words, x_scales, w1, gs, d_words, d_scales, mem, res, gn, w2, offs, n1, n2, kidx, n3, out
+):
+    nc = tc.nc
+    with ExitStack() as ctx:
+        lists = ctx.enter_context(tc.tile_pool(name="lists", bufs=1))
+        keep = ctx.enter_context(tc.tile_pool(name="keep", bufs=1))
+        psum = ctx.enter_context(tc.psum_pool(name="psum", bufs=1))
+
+        def sb(name, shape, dtype):
+            return keep.tile(shape, dtype, name=name, align_bytes=64)
+
+        def load_list(name, src):
+            tl = lists.tile([P, S // 16], U16, name=name)
+            nc.sync.dma_start(tl[:], src)
+            return tl
+
+        xs_win = sb("xs_win", [P, T], U8)
+        ds_win = sb("ds_win", [P, G], U8)
+        d_scale = sb("d_scale", [P, H], U8)
+        y_win = [sb("y_win%d" % t, [P, 2 * S], F32) for t in range(PACK)]
+        warm = sb("warm", [P, 16], F32)
+        nc.gpsimd.memset(xs_win[:].bitcast(I32), 0)
+        nc.vector.memset(ds_win[:].bitcast(I32), 0)
+        nc.vector.memset(d_scale[:].bitcast(I32), 0)
+        for t in range(PACK):
+            nc.vector.memset(y_win[t][:, S:], 0.0)
+        nc.scalar.activation(warm[:, 0:1], y_win[0][:, S : S + 1], ACT.Sigmoid)
+
+        offs_t = load_list("offs_t", offs)
+        xw_win = sb("xw_win", [P, T], I32)
+        nc.sync.dma_start(xw_win[:], x_words[0].rearrange("p c r -> p (c r)").bitcast(I32))
+        for q in range(4):
+            nc.sync.dma_start(xs_win[32 * q : 32 * q + 4, :].bitcast(I32), x_scales[0, 4 * q : 4 * q + 4, :].bitcast(I32))
+        w1_raw = [sb("w1_raw%d" % h, [P, PACK, H // 2], F32) for h in range(2)]
+        w1_rows = w1.rearrange("(p j) c -> p j c", j=PACK)
+        for h in range(2):
+            nc.sync.dma_start(w1_raw[h][:], w1_rows[:, :, h * (H // 2) : (h + 1) * (H // 2)])
+        dw_win = sb("dw_win", [P, G], I32)
+        nc.sync.dma_start(dw_win[:], d_words[0].rearrange("p c r -> p (c r)").bitcast(I32))
+        kidx_t = load_list("kidx_t", kidx)
+        n1_t = load_list("n1_t", n1)
+        n2_t = load_list("n2_t", n2)
+        n3_t = load_list("n3_t", n3)
+        gs_t = sb("gs_t", [P, PACK], F32)
+        nc.gpsimd.dma_start(gs_t[:], gs.rearrange("(p t) o -> p (t o)", t=PACK))
+        nc.gpsimd.dma_start(ds_win[0:P:8, :].bitcast(I32), d_scales[0].bitcast(I32))
+        page = [sb("page%d" % t, [P, U], F32) for t in range(PACK)]
+        mem_rows = mem.rearrange("(a t b) u -> t a b u", t=PACK, b=8)
+        for t in range(PACK):
+            nc.sync.dma_start(page[t][:], mem_rows[t])
+        w2_raw = sb("w2_raw", [P, PACK, N], F32)
+        w2_rows = w2.rearrange("(a t b) n -> t a b n", t=PACK, b=8)
+        for t in range(PACK):
+            nc.sync.dma_start(w2_raw[:, t, :], w2_rows[t])
+        gn_t = [sb("gn_t%d" % t, [P, 1], F32) for t in range(PACK)]
+        with nc.allow_non_contiguous_dma(reason="512 row factors, one value a row"):
+            for t in range(PACK):
+                nc.gpsimd.dma_start(gn_t[t][:], gn.rearrange("(a t b) o -> t a b o", t=PACK, b=8)[t])
+        res_t = sb("res_t", [P, PACK, U], F32)
+        nc.sync.dma_start(res_t[:], res.rearrange("(m p) u -> p m u", p=P))
+
+        x_code = sb("x_code", [P, S], U32)
+        x_scale = sb("x_scale", [P, S], U8)
+        nc.vector.tensor_copy(x_code[:], xw_win[:].bitcast(U32).indirect(offs_t[:]))
+        nc.vector.tensor_copy(x_scale[:], xs_win[:].indirect(offs_t[:]))
+
+        w1_bf = sb("w1_bf", [P, H * PACK], BF16)
+        w1_dst = w1_bf[:].rearrange("p (t m j) -> p m j t", t=PACK, j=PACK)
+        half = P // 2
+        nc.scalar.copy(w1_dst[:, 0:half], w1_raw[0][:].rearrange("p j (m t) -> p m j t", t=PACK))
+        nc.vector.tensor_copy(w1_dst[:, half:P], w1_raw[1][:].rearrange("p j (m t) -> p m j t", t=PACK))
+        w1_code = sb("w1_code", [P, H], U32)
+        w1_scale = sb("w1_scale", [P, H], U8)
+        for h in range(2):
+            cols = slice(h * (H // 2), (h + 1) * (H // 2))
+            nc.vector.quantize_mx(
+                out=w1_code[:, cols].bitcast(FP8X4),
+                scales=w1_scale[:, cols],
+                in_=w1_bf[:, h * 2 * H : (h + 1) * 2 * H],
+            )
+        y_ps = []
+        for t in range(PACK):
+            acc = psum.tile([P, S], F32, name="y_ps%d" % t, tag="bank%d" % t)
+            cols = slice(t * P, (t + 1) * P)
+            nc.tensor.matmul_mx(
+                out=acc[:], lhsT=w1_code[:, cols].bitcast(FP8X4), lhsT_scale=w1_scale[:, cols],
+                rhs=x_code[:].bitcast(FP8X4), rhs_scale=x_scale[:], start=True, stop=True,
+            )
+            y_ps.append(acc)
+
+        d_pick = sb("d_pick", [P, H], U32)
+        ds_pick = sb("ds_pick", [P, H], U8)
+        d_code = sb("d_code", [P, H], U32)
+        ds_dealt = sb("ds_dealt", [P, H], U8)
+        nc.vector.tensor_copy(d_pick[:], dw_win[:].bitcast(U32).indirect(kidx_t[:]))
+        nc.vector.tensor_copy(ds_pick[:], ds_win[:].indirect(kidx_t[:]))
+        nc.vector.tensor_copy(
+            d_code[:].rearrange("p (t a b) -> p a t b", t=PACK, b=8),
+            d_pick[:].rearrange("p (a t b) -> p a t b", t=PACK, b=8),
+        )
+        nc.vector.tensor_copy(
+            ds_dealt[:].bitcast(I32).rearrange("p (t a b) -> p t a b", t=PACK, b=2),
+            ds_pick[:].bitcast(I32).rearrange("p (a t b) -> p t a b", t=PACK, b=2),
+        )
+        for r in range(4):
+            nc.sync.dma_start(d_scale[r:P:32, :].bitcast(I32), ds_dealt[8 * r : P : 32, :].bitcast(I32))
+
+        near = sb("near", [P, PACK, S], F32)
+        stay = sb("stay", [P, PACK, S], F32)
+        held = []
+        for t in range(PACK):
+            nc.scalar.copy(y_win[t][:, 0:S], y_ps[t][:])
+            sig = sb("sig%d" % t, [P, S], F32)
+            nc.scalar.activation(sig[:], y_win[t][:].indirect(n1_t[:]), ACT.Sigmoid)
+            gate = sb("gate%d" % t, [P, S], F32)
+            nc.scalar.activation(gate[:], sig[:], ACT.Copy, scale=gs_t[:, t : t + 1])
+            old = sb("held%d" % t, [P, S], F32)
+            nc.vector.tensor_scalar(old[:], page[t][:].indirect(n3_t[:]), 0.5, 0.0, ALU.mult, ALU.add)
+            held.append(old)
+            nc.vector.tensor_tensor(near[:, t, :], y_win[t][:].indirect(n2_t[:]), gate[:], ALU.mult)
+            nc.vector.scalar_tensor_tensor(
+                stay[:, t, :], gate[:], gs_t[:, t : t + 1], y_ps[t][:], ALU.subtract, ALU.mult
+            )
+        z_bf = sb("z_bf", [P, S * PACK], BF16)
+        nc.vector.tensor_tensor(
+            z_bf[:].rearrange("p (c i t) -> p c t i", i=4, t=PACK),
+            near[:].rearrange("p t (c i) -> p c t i", i=4),
+            stay[:].rearrange("p t (c i) -> p c t i", i=4),
+            ALU.subtract,
+        )
+
+        w2_bf = sb("w2_bf", [P, N * PACK], BF16)
+        nc.scalar.copy(
+            w2_bf[:].rearrange("p (c i t) -> p c t i", i=4, t=PACK),
+            w2_raw[:].rearrange("p t (c i) -> p c t i", i=4),
+        )
+        z_code = sb("z_code", [P, S], U32)
+        z_scale = sb("z_scale", [P, S], U8)
+        nc.vector.quantize_mx(out=z_code[:].bitcast(FP8X4), scales=z_scale[:], in_=z_bf[:])
+        w2_code = sb("w2_code", [P, N], U32)
+        w2_scale = sb("w2_scale", [P, N], U8)
+        nc.vector.quantize_mx(out=w2_code[:].bitcast(FP8X4), scales=w2_scale[:], in_=w2_bf[:])
+
+        chunks = U // CHUNK
+        z2_bf = [sb("z2_bf%d" % c, [P, CHUNK, PACK], BF16) for c in range(chunks)]
+        for t in range(PACK):
+            acc = psum.tile([P, S], F32, name="s_ps%d" % t, tag="bank%d" % (PACK + t))
+            cols = slice(t * P, (t + 1) * P)
+            nc.tensor.matmul_mx(
+                out=acc[:], lhsT=d_code[:, cols].bitcast(FP8X4), lhsT_scale=d_scale[:, cols],
+                rhs=z_code[:].bitcast(FP8X4), rhs_scale=z_scale[:], start=True, stop=True,
+            )
+            new = sb("new%d" % t, [P, S], F32)
+            nc.vector.scalar_tensor_tensor(new[:], acc[:], 0.0625, held[t][:], ALU.mult, ALU.max)
+            nc.vector.tensor_copy(page[t][:].indirect(n3_t[:]), new[:])
+            for c in range(chunks):
+                nc.scalar.activation(
+                    z2_bf[c][:, :, t], page[t][:, c * CHUNK : (c + 1) * CHUNK], ACT.Copy, scale=gn_t[t][:]
+                )
+
+        out_rows = out.rearrange("(m p) u -> p m u", p=P)
+        for c in range(chunks):
+            slots = slice(c * CHUNK, (c + 1) * CHUNK)
+            z2_code = sb("z2_code%d" % c, [P, CHUNK], U32)
+            z2_scale = sb("z2_scale%d" % c, [P, CHUNK], U8)
+            nc.vector.quantize_mx(
+                out=z2_code[:].bitcast(FP8X4), scales=z2_scale[:], in_=z2_bf[c][:].rearrange("p c t -> p (c t)")
+            )
+            for pair in range(2):
+                acc = psum.tile([P, 2, CHUNK], F32, name="o_ps%d_%d" % (c, pair), tag="bank%d" % (2 * c + pair))
+                for i in range(2):
+                    cols = slice((2 * pair + i) * P, (2 * pair + i + 1) * P)
+                    nc.tensor.matmul_mx(
+                        out=acc[:, i, :], lhsT=w2_code[:, cols].bitcast(FP8X4), lhsT_scale=w2_scale[:, cols],
+                        rhs=z2_code[:].bitcast(FP8X4), rhs_scale=z2_scale[:], start=True, stop=True,
+                    )
+                done = sb("done%d_%d" % (c, pair), [P, 2, CHUNK], F32)
+                nc.vector.tensor_tensor(done[:], acc[:], res_t[:, 2 * pair : 2 * pair + 2, slots], ALU.add)
+                nc.sync.dma_start(out_rows[:, 2 * pair : 2 * pair + 2, slots], done[:])

@@ -27,10 +27,11 @@ def tile_picked_pqktrackpagex_none_p_kernel(
     with ExitStack() as ctx:
         lists = ctx.enter_context(tc.tile_pool(name="lists", bufs=1))
         keep = ctx.enter_context(tc.tile_pool(name="keep", bufs=1))
+        ring = ctx.enter_context(tc.tile_pool(name="ring", bufs=2))
         psum = ctx.enter_context(tc.psum_pool(name="psum", bufs=1))
 
-        def sb(name, shape, dtype):
-            return keep.tile(shape, dtype, name=name, align_bytes=64)
+        def sb(name, shape, dtype, over=None):
+            return keep.tile(shape, dtype, name=name, tag=over or name, align_bytes=64)
 
         def load_list(name, src):
             tl = lists.tile([P, S // 16], U16, name=name)
@@ -54,22 +55,21 @@ def tile_picked_pqktrackpagex_none_p_kernel(
         nc.sync.dma_start(xw_win[:], x_words[0].rearrange("p c r -> p (c r)").bitcast(I32))
         for q in range(4):
             nc.sync.dma_start(xs_win[32 * q : 32 * q + 4, :].bitcast(I32), x_scales[0, 4 * q : 4 * q + 4, :].bitcast(I32))
-        w1_raw = [sb("w1_raw%d" % h, [P, PACK, H // 2], F32) for h in range(2)]
-        w1_rows = w1.rearrange("(p j) c -> p j c", j=PACK)
-        for h in range(2):
-            nc.sync.dma_start(w1_raw[h][:], w1_rows[:, :, h * (H // 2) : (h + 1) * (H // 2)])
+        kidx_t = load_list("kidx_t", kidx)
         dw_win = sb("dw_win", [P, G], I32)
         nc.sync.dma_start(dw_win[:], d_words[0].rearrange("p c r -> p (c r)").bitcast(I32))
-        kidx_t = load_list("kidx_t", kidx)
-        n1_t = load_list("n1_t", n1)
-        n2_t = load_list("n2_t", n2)
+        nc.sync.dma_start(ds_win[0:P:8, :].bitcast(I32), d_scales[0].bitcast(I32))
+        w1_raw = sb("w1_raw", [P, PACK, H], F32)
+        nc.sync.dma_start(w1_raw[:], w1.rearrange("(p j) c -> p j c", j=PACK))
         n3_t = load_list("n3_t", n3)
-        gs_t = sb("gs_t", [P, PACK], F32)
-        nc.gpsimd.dma_start(gs_t[:], gs.rearrange("(p t) o -> p (t o)", t=PACK))
-        nc.gpsimd.dma_start(ds_win[0:P:8, :].bitcast(I32), d_scales[0].bitcast(I32))
         page = [sb("page%d" % t, [P, U], F32) for t in range(PACK)]
         mem_rows = mem.rearrange("(a t b) u -> t a b u", t=PACK, b=8)
-        for t in range(PACK):
+        nc.sync.dma_start(page[0][:], mem_rows[0])
+        n1_t = load_list("n1_t", n1)
+        n2_t = load_list("n2_t", n2)
+        gs_t = sb("gs_t", [P, PACK], F32)
+        nc.sync.dma_start(gs_t[:], gs.rearrange("(p t) o -> p (t o)", t=PACK))
+        for t in range(1, PACK):
             nc.sync.dma_start(page[t][:], mem_rows[t])
         w2_raw = sb("w2_raw", [P, PACK, N], F32)
         w2_rows = w2.rearrange("(a t b) n -> t a b n", t=PACK, b=8)
@@ -78,20 +78,51 @@ def tile_picked_pqktrackpagex_none_p_kernel(
         gn_t = [sb("gn_t%d" % t, [P, 1], F32) for t in range(PACK)]
         with nc.allow_non_contiguous_dma(reason="512 row factors, one value a row"):
             for t in range(PACK):
-                nc.gpsimd.dma_start(gn_t[t][:], gn.rearrange("(a t b) o -> t a b o", t=PACK, b=8)[t])
-        res_t = sb("res_t", [P, PACK, U], F32)
-        nc.sync.dma_start(res_t[:], res.rearrange("(m p) u -> p m u", p=P))
+                nc.sync.dma_start(gn_t[t][:], gn.rearrange("(a t b) o -> t a b o", t=PACK, b=8)[t])
+        chunks = U // CHUNK
+        res_rows = res.rearrange("(m p) u -> p m u", p=P)
+        res_t = []
+        for c in range(chunks):
+            part = keep.tile([P, PACK, CHUNK], F32, name="res_t%d" % c, tag="res%d" % c, align_bytes=64)
+            nc.sync.dma_start(part[:], res_rows[:, :, c * CHUNK : (c + 1) * CHUNK])
+            res_t.append(part)
 
         x_code = sb("x_code", [P, S], U32)
         x_scale = sb("x_scale", [P, S], U8)
         nc.vector.tensor_copy(x_code[:], xw_win[:].bitcast(U32).indirect(offs_t[:]))
         nc.vector.tensor_copy(x_scale[:], xs_win[:].indirect(offs_t[:]))
 
+        held = []
+
+        def fetch_held(over):
+            t = len(held)
+            old = sb("held%d" % t, [P, S], F32, over=over)
+            nc.vector.tensor_scalar(old[:], page[t][:].indirect(n3_t[:]), 0.5, 0.0, ALU.mult, ALU.add)
+            held.append(old)
+
+        d_pick = sb("d_pick", [P, H], U32)
+        ds_pick = sb("ds_pick", [P, H], U8)
+        d_code = sb("d_code", [P, H], U32)
+        ds_dealt = sb("ds_dealt", [P, H], U8)
+        nc.vector.tensor_copy(d_pick[:], dw_win[:].bitcast(U32).indirect(kidx_t[:]))
+        nc.vector.tensor_copy(ds_pick[:], ds_win[:].indirect(kidx_t[:]))
+        nc.vector.tensor_copy(
+            d_code[:].rearrange("p (t a b) -> p a t b", t=PACK, b=8),
+            d_pick[:].rearrange("p (a t b) -> p a t b", t=PACK, b=8),
+        )
+        nc.vector.tensor_copy(
+            ds_dealt[:].bitcast(I32).rearrange("p (t a b) -> p t a b", t=PACK, b=2),
+            ds_pick[:].bitcast(I32).rearrange("p (a t b) -> p t a b", t=PACK, b=2),
+        )
+        for r in range(4):
+            nc.sync.dma_start(d_scale[r:P:32, :].bitcast(I32), ds_dealt[8 * r : P : 32, :].bitcast(I32))
+
         w1_bf = sb("w1_bf", [P, H * PACK], BF16)
         w1_dst = w1_bf[:].rearrange("p (t m j) -> p m j t", t=PACK, j=PACK)
-        half = P // 2
-        nc.scalar.copy(w1_dst[:, 0:half], w1_raw[0][:].rearrange("p j (m t) -> p m j t", t=PACK))
-        nc.vector.tensor_copy(w1_dst[:, half:P], w1_raw[1][:].rearrange("p j (m t) -> p m j t", t=PACK))
+        half = 96
+        w1_src = w1_raw[:].rearrange("p j (m t) -> p m j t", t=PACK)
+        nc.scalar.copy(w1_dst[:, 0:half], w1_src[:, 0:half])
+        nc.vector.tensor_copy(w1_dst[:, half:P], w1_src[:, half:P])
         w1_code = sb("w1_code", [P, H], U32)
         w1_scale = sb("w1_scale", [P, H], U8)
         for h in range(2):
@@ -111,35 +142,17 @@ def tile_picked_pqktrackpagex_none_p_kernel(
             )
             y_ps.append(acc)
 
-        d_pick = sb("d_pick", [P, H], U32)
-        ds_pick = sb("ds_pick", [P, H], U8)
-        d_code = sb("d_code", [P, H], U32)
-        ds_dealt = sb("ds_dealt", [P, H], U8)
-        nc.vector.tensor_copy(d_pick[:], dw_win[:].bitcast(U32).indirect(kidx_t[:]))
-        nc.vector.tensor_copy(ds_pick[:], ds_win[:].indirect(kidx_t[:]))
-        nc.vector.tensor_copy(
-            d_code[:].rearrange("p (t a b) -> p a t b", t=PACK, b=8),
-            d_pick[:].rearrange("p (a t b) -> p a t b", t=PACK, b=8),
-        )
-        nc.vector.tensor_copy(
-            ds_dealt[:].bitcast(I32).rearrange("p (t a b) -> p t a b", t=PACK, b=2),
-            ds_pick[:].bitcast(I32).rearrange("p (a t b) -> p t a b", t=PACK, b=2),
-        )
-        for r in range(4):
-            nc.sync.dma_start(d_scale[r:P:32, :].bitcast(I32), ds_dealt[8 * r : P : 32, :].bitcast(I32))
+        for t in range(PACK - 1):
+            fetch_held(None)
 
         near = sb("near", [P, PACK, S], F32)
         stay = sb("stay", [P, PACK, S], F32)
-        held = []
         for t in range(PACK):
             nc.scalar.copy(y_win[t][:, 0:S], y_ps[t][:])
             sig = sb("sig%d" % t, [P, S], F32)
             nc.scalar.activation(sig[:], y_win[t][:].indirect(n1_t[:]), ACT.Sigmoid)
             gate = sb("gate%d" % t, [P, S], F32)
             nc.scalar.activation(gate[:], sig[:], ACT.Copy, scale=gs_t[:, t : t + 1])
-            old = sb("held%d" % t, [P, S], F32)
-            nc.vector.tensor_scalar(old[:], page[t][:].indirect(n3_t[:]), 0.5, 0.0, ALU.mult, ALU.add)
-            held.append(old)
             nc.vector.tensor_tensor(near[:, t, :], y_win[t][:].indirect(n2_t[:]), gate[:], ALU.mult)
             nc.vector.scalar_tensor_tensor(
                 stay[:, t, :], gate[:], gs_t[:, t : t + 1], y_ps[t][:], ALU.subtract, ALU.mult
@@ -160,12 +173,9 @@ def tile_picked_pqktrackpagex_none_p_kernel(
         z_code = sb("z_code", [P, S], U32)
         z_scale = sb("z_scale", [P, S], U8)
         nc.vector.quantize_mx(out=z_code[:].bitcast(FP8X4), scales=z_scale[:], in_=z_bf[:])
-        w2_code = sb("w2_code", [P, N], U32)
-        w2_scale = sb("w2_scale", [P, N], U8)
-        nc.vector.quantize_mx(out=w2_code[:].bitcast(FP8X4), scales=w2_scale[:], in_=w2_bf[:])
+        fetch_held("z_bf")
 
-        chunks = U // CHUNK
-        z2_bf = [sb("z2_bf%d" % c, [P, CHUNK, PACK], BF16) for c in range(chunks)]
+        z2_bf = sb("z2_bf", [P, U, PACK], BF16)
         for t in range(PACK):
             acc = psum.tile([P, S], F32, name="s_ps%d" % t, tag="bank%d" % (PACK + t))
             cols = slice(t * P, (t + 1) * P)
@@ -173,21 +183,27 @@ def tile_picked_pqktrackpagex_none_p_kernel(
                 out=acc[:], lhsT=d_code[:, cols].bitcast(FP8X4), lhsT_scale=d_scale[:, cols],
                 rhs=z_code[:].bitcast(FP8X4), rhs_scale=z_scale[:], start=True, stop=True,
             )
-            new = sb("new%d" % t, [P, S], F32)
+            new = ring.tile([P, S], F32, name="new", align_bytes=64)
             nc.vector.scalar_tensor_tensor(new[:], acc[:], 0.0625, held[t][:], ALU.mult, ALU.max)
             nc.vector.tensor_copy(page[t][:].indirect(n3_t[:]), new[:])
-            for c in range(chunks):
+            width = CHUNK if t == PACK - 1 else U
+            for c0 in range(0, U, width):
                 nc.scalar.activation(
-                    z2_bf[c][:, :, t], page[t][:, c * CHUNK : (c + 1) * CHUNK], ACT.Copy, scale=gn_t[t][:]
+                    z2_bf[:, c0 : c0 + width, t], page[t][:, c0 : c0 + width], ACT.Copy, scale=gn_t[t][:]
                 )
+
+        w2_code = ring.tile([P, N], U32, name="w2_code", tag="new", align_bytes=64)
+        w2_scale = sb("w2_scale", [P, N], U8)
+        nc.vector.quantize_mx(out=w2_code[:].bitcast(FP8X4), scales=w2_scale[:], in_=w2_bf[:])
 
         out_rows = out.rearrange("(m p) u -> p m u", p=P)
         for c in range(chunks):
             slots = slice(c * CHUNK, (c + 1) * CHUNK)
-            z2_code = sb("z2_code%d" % c, [P, CHUNK], U32)
+            tag = "res%d" % (c - 2) if c >= 2 else "z2_code%d" % c
+            z2_code = keep.tile([P, CHUNK], U32, name="z2_code%d" % c, tag=tag, align_bytes=64)
             z2_scale = sb("z2_scale%d" % c, [P, CHUNK], U8)
             nc.vector.quantize_mx(
-                out=z2_code[:].bitcast(FP8X4), scales=z2_scale[:], in_=z2_bf[c][:].rearrange("p c t -> p (c t)")
+                out=z2_code[:].bitcast(FP8X4), scales=z2_scale[:], in_=z2_bf[:, slots, :].rearrange("p c t -> p (c t)")
             )
             for pair in range(2):
                 acc = psum.tile([P, 2, CHUNK], F32, name="o_ps%d_%d" % (c, pair), tag="bank%d" % (2 * c + pair))
@@ -198,5 +214,5 @@ def tile_picked_pqktrackpagex_none_p_kernel(
                         rhs=z2_code[:].bitcast(FP8X4), rhs_scale=z2_scale[:], start=True, stop=True,
                     )
                 done = sb("done%d_%d" % (c, pair), [P, 2, CHUNK], F32)
-                nc.vector.tensor_tensor(done[:], acc[:], res_t[:, 2 * pair : 2 * pair + 2, slots], ALU.add)
+                nc.vector.tensor_tensor(done[:], acc[:], res_t[c][:, 2 * pair : 2 * pair + 2, :], ALU.add)
                 nc.sync.dma_start(out_rows[:, 2 * pair : 2 * pair + 2, slots], done[:])

@@ -27,7 +27,6 @@ def tile_picked_pqktrackpagex_none_p_kernel(
     with ExitStack() as ctx:
         lists = ctx.enter_context(tc.tile_pool(name="lists", bufs=1))
         keep = ctx.enter_context(tc.tile_pool(name="keep", bufs=1))
-        ring = ctx.enter_context(tc.tile_pool(name="ring", bufs=2))
         psum = ctx.enter_context(tc.psum_pool(name="psum", bufs=1))
 
         def sb(name, shape, dtype, over=None):
@@ -158,21 +157,28 @@ def tile_picked_pqktrackpagex_none_p_kernel(
                 stay[:, t, :], gate[:], gs_t[:, t : t + 1], y_ps[t][:], ALU.subtract, ALU.mult
             )
         z_bf = sb("z_bf", [P, S * PACK], BF16)
-        nc.vector.tensor_tensor(
-            z_bf[:].rearrange("p (c i t) -> p c t i", i=4, t=PACK),
-            near[:].rearrange("p t (c i) -> p c t i", i=4),
-            stay[:].rearrange("p t (c i) -> p c t i", i=4),
-            ALU.subtract,
-        )
+        z_dst = z_bf[:].rearrange("p (c i t) -> p c t i", i=2, t=PACK)
+        for h in range(2):
+            pairs = slice(h * (S // 4), (h + 1) * (S // 4))
+            nc.vector.tensor_tensor(
+                z_dst[:, pairs],
+                near[:].rearrange("p t (c i) -> p c t i", i=2)[:, pairs],
+                stay[:].rearrange("p t (c i) -> p c t i", i=2)[:, pairs],
+                ALU.subtract,
+            )
 
-        w2_bf = sb("w2_bf", [P, N * PACK], BF16)
+        w2_bf = sb("w2_bf", [P, N * PACK], BF16, over="sig3")
         nc.scalar.copy(
             w2_bf[:].rearrange("p (c i t) -> p c t i", i=4, t=PACK),
             w2_raw[:].rearrange("p t (c i) -> p c t i", i=4),
         )
         z_code = sb("z_code", [P, S], U32)
         z_scale = sb("z_scale", [P, S], U8)
-        nc.vector.quantize_mx(out=z_code[:].bitcast(FP8X4), scales=z_scale[:], in_=z_bf[:])
+        for h in range(2):
+            cols = slice(h * (S // 2), (h + 1) * (S // 2))
+            nc.vector.quantize_mx(
+                out=z_code[:, cols].bitcast(FP8X4), scales=z_scale[:, cols], in_=z_bf[:, h * 2 * S : (h + 1) * 2 * S]
+            )
         fetch_held("z_bf")
 
         z2_bf = sb("z2_bf", [P, U, PACK], BF16)
@@ -183,7 +189,7 @@ def tile_picked_pqktrackpagex_none_p_kernel(
                 out=acc[:], lhsT=d_code[:, cols].bitcast(FP8X4), lhsT_scale=d_scale[:, cols],
                 rhs=z_code[:].bitcast(FP8X4), rhs_scale=z_scale[:], start=True, stop=True,
             )
-            new = ring.tile([P, S], F32, name="new", align_bytes=64)
+            new = sb("new%d" % t, [P, S], F32)
             nc.vector.scalar_tensor_tensor(new[:], acc[:], 0.0625, held[t][:], ALU.mult, ALU.max)
             nc.vector.tensor_copy(page[t][:].indirect(n3_t[:]), new[:])
             width = CHUNK if t == PACK - 1 else U
@@ -192,7 +198,7 @@ def tile_picked_pqktrackpagex_none_p_kernel(
                     z2_bf[:, c0 : c0 + width, t], page[t][:, c0 : c0 + width], ACT.Copy, scale=gn_t[t][:]
                 )
 
-        w2_code = ring.tile([P, N], U32, name="w2_code", tag="new", align_bytes=64)
+        w2_code = sb("w2_code", [P, N], U32, over="new2")
         w2_scale = sb("w2_scale", [P, N], U8)
         nc.vector.quantize_mx(out=w2_code[:].bitcast(FP8X4), scales=w2_scale[:], in_=w2_bf[:])
 

@@ -101,24 +101,12 @@ def tile_picked_pqktrackpagex_none_p_kernel(
 
         d_pick = sb("d_pick", [P, H], U32)
         ds_pick = sb("ds_pick", [P, H], U8)
-        d_code = sb("d_code", [P, H], U32)
-        ds_dealt = sb("ds_dealt", [P, H], U8)
         nc.vector.tensor_copy(d_pick[:], dw_win[:].bitcast(U32).indirect(kidx_t[:]))
         nc.vector.tensor_copy(ds_pick[:], ds_win[:].indirect(kidx_t[:]))
-        nc.vector.tensor_copy(
-            d_code[:].rearrange("p (t a b) -> p a t b", t=PACK, b=8),
-            d_pick[:].rearrange("p (a t b) -> p a t b", t=PACK, b=8),
-        )
-        nc.vector.tensor_copy(
-            ds_dealt[:].bitcast(I32).rearrange("p (t a b) -> p t a b", t=PACK, b=2),
-            ds_pick[:].bitcast(I32).rearrange("p (a t b) -> p t a b", t=PACK, b=2),
-        )
-        for r in range(4):
-            nc.sync.dma_start(d_scale[r:P:32, :].bitcast(I32), ds_dealt[8 * r : P : 32, :].bitcast(I32))
 
         w1_bf = sb("w1_bf", [P, H * PACK], BF16)
         w1_dst = w1_bf[:].rearrange("p (t m j) -> p m j t", t=PACK, j=PACK)
-        half = 96
+        half = 72
         w1_src = w1_raw[:].rearrange("p j (m t) -> p m j t", t=PACK)
         nc.scalar.copy(w1_dst[:, 0:half], w1_src[:, 0:half])
         nc.vector.tensor_copy(w1_dst[:, half:P], w1_src[:, half:P])
@@ -141,6 +129,19 @@ def tile_picked_pqktrackpagex_none_p_kernel(
             )
             y_ps.append(acc)
 
+        d_code = sb("d_code", [P, H], U32, over="w1_bf")
+        ds_dealt = sb("ds_dealt", [P, H], U8, over="w1_raw")
+        nc.vector.tensor_copy(
+            d_code[:].rearrange("p (t a b) -> p a t b", t=PACK, b=8),
+            d_pick[:].rearrange("p (a t b) -> p a t b", t=PACK, b=8),
+        )
+        nc.vector.tensor_copy(
+            ds_dealt[:].bitcast(I32).rearrange("p (t a b) -> p t a b", t=PACK, b=2),
+            ds_pick[:].bitcast(I32).rearrange("p (a t b) -> p t a b", t=PACK, b=2),
+        )
+        for r in range(4):
+            nc.sync.dma_start(d_scale[r:P:32, :].bitcast(I32), ds_dealt[8 * r : P : 32, :].bitcast(I32))
+
         for t in range(PACK - 1):
             fetch_held(None)
 
@@ -152,7 +153,9 @@ def tile_picked_pqktrackpagex_none_p_kernel(
             nc.scalar.activation(sig[:], y_win[t][:].indirect(n1_t[:]), ACT.Sigmoid)
             gate = sb("gate%d" % t, [P, S], F32)
             nc.scalar.activation(gate[:], sig[:], ACT.Copy, scale=gs_t[:, t : t + 1])
-            nc.vector.tensor_tensor(near[:, t, :], y_win[t][:].indirect(n2_t[:]), gate[:], ALU.mult)
+            other = sb("other%d" % t, [P, S], F32)
+            nc.vector.tensor_copy(other[:], y_win[t][:].indirect(n2_t[:]))
+            nc.gpsimd.tensor_tensor(near[:, t, :], other[:], gate[:], ALU.mult)
             nc.vector.scalar_tensor_tensor(
                 stay[:, t, :], gate[:], gs_t[:, t : t + 1], y_ps[t][:], ALU.subtract, ALU.mult
             )

@@ -80,11 +80,12 @@ def tile_picked_pqktrackpagex_none_p_kernel(
                 nc.sync.dma_start(gn_t[t][:], gn.rearrange("(a t b) o -> t a b o", t=PACK, b=8)[t])
         chunks = U // CHUNK
         res_rows = res.rearrange("(m p) u -> p m u", p=P)
-        res_t = []
+        res_t = {}
         for c in range(chunks):
-            part = keep.tile([P, PACK, CHUNK], F32, name="res_t%d" % c, tag="res%d" % c, align_bytes=64)
-            nc.sync.dma_start(part[:], res_rows[:, :, c * CHUNK : (c + 1) * CHUNK])
-            res_t.append(part)
+            for pair in range(2):
+                part = sb("res%d_%d" % (c, pair), [P, 2, CHUNK], F32)
+                nc.sync.dma_start(part[:], res_rows[:, 2 * pair : 2 * pair + 2, c * CHUNK : (c + 1) * CHUNK])
+                res_t[c, pair] = part
 
         x_code = sb("x_code", [P, S], U32)
         x_scale = sb("x_scale", [P, S], U8)
@@ -152,7 +153,7 @@ def tile_picked_pqktrackpagex_none_p_kernel(
             sig = sb("sig%d" % t, [P, S], F32)
             nc.scalar.activation(sig[:], y_win[t][:].indirect(n1_t[:]), ACT.Sigmoid)
             gate = sb("gate%d" % t, [P, S], F32)
-            nc.scalar.activation(gate[:], sig[:], ACT.Copy, scale=gs_t[:, t : t + 1])
+            nc.gpsimd.tensor_scalar(gate[:], sig[:], gs_t[:, t : t + 1], 0.0, ALU.mult, ALU.add)
             other = sb("other%d" % t, [P, S], F32)
             nc.vector.tensor_copy(other[:], y_win[t][:].indirect(n2_t[:]))
             nc.gpsimd.tensor_tensor(near[:, t, :], other[:], gate[:], ALU.mult)
@@ -184,7 +185,7 @@ def tile_picked_pqktrackpagex_none_p_kernel(
             )
         fetch_held("z_bf")
 
-        z2_bf = sb("z2_bf", [P, U, PACK], BF16)
+        scores = []
         for t in range(PACK):
             acc = psum.tile([P, S], F32, name="s_ps%d" % t, tag="bank%d" % (PACK + t))
             cols = slice(t * P, (t + 1) * P)
@@ -192,9 +193,25 @@ def tile_picked_pqktrackpagex_none_p_kernel(
                 out=acc[:], lhsT=d_code[:, cols].bitcast(FP8X4), lhsT_scale=d_scale[:, cols],
                 rhs=z_code[:].bitcast(FP8X4), rhs_scale=z_scale[:], start=True, stop=True,
             )
-            new = sb("new%d" % t, [P, S], F32)
-            nc.vector.scalar_tensor_tensor(new[:], acc[:], 0.0625, held[t][:], ALU.mult, ALU.max)
-            nc.vector.tensor_copy(page[t][:].indirect(n3_t[:]), new[:])
+            scores.append(acc)
+        new = []
+        for t in range(PACK):
+            top = sb("new%d" % t, [P, S], F32)
+            if t < 2:
+                nc.vector.scalar_tensor_tensor(top[:], scores[t][:], 0.0625, held[t][:], ALU.mult, ALU.max)
+            else:
+                score = sb("score%d" % t, [P, S], F32)
+                nc.scalar.activation(score[:], scores[t][:], ACT.Copy, scale=0.0625)
+                gap = sb("gap%d" % t, [P, S], F32)
+                nc.gpsimd.tensor_tensor(gap[:], score[:], held[t][:], ALU.subtract)
+                nc.scalar.activation(top[:], gap[:], ACT.Relu)
+            new.append(top)
+        z2_bf = sb("z2_bf", [P, U, PACK], BF16, over="gap3")
+        for t in range(PACK):
+            if t < 2:
+                nc.vector.tensor_copy(page[t][:].indirect(n3_t[:]), new[t][:])
+            else:
+                nc.vector.tensor_tensor(page[t][:].indirect(n3_t[:]), held[t][:], new[t][:], ALU.add)
             width = CHUNK if t == PACK - 1 else U
             for c0 in range(0, U, width):
                 nc.scalar.activation(
@@ -206,22 +223,35 @@ def tile_picked_pqktrackpagex_none_p_kernel(
         nc.vector.quantize_mx(out=w2_code[:].bitcast(FP8X4), scales=w2_scale[:], in_=w2_bf[:])
 
         out_rows = out.rearrange("(m p) u -> p m u", p=P)
+
+        def store(c, pair, done):
+            nc.sync.dma_start(out_rows[:, 2 * pair : 2 * pair + 2, c * CHUNK : (c + 1) * CHUNK], done[:])
+
+        aside = (1, 1)
+        banks = {}
         for c in range(chunks):
             slots = slice(c * CHUNK, (c + 1) * CHUNK)
-            tag = "res%d" % (c - 2) if c >= 2 else "z2_code%d" % c
-            z2_code = keep.tile([P, CHUNK], U32, name="z2_code%d" % c, tag=tag, align_bytes=64)
+            z2_code = sb("z2_code%d" % c, [P, CHUNK], U32, over="res0_%d" % (c - 2) if c >= 2 else None)
             z2_scale = sb("z2_scale%d" % c, [P, CHUNK], U8)
             nc.vector.quantize_mx(
                 out=z2_code[:].bitcast(FP8X4), scales=z2_scale[:], in_=z2_bf[:, slots, :].rearrange("p c t -> p (c t)")
             )
+            if c == chunks - 1:
+                sums = sb("sums", [P, 2, CHUNK], F32, over="gap3")
+                nc.scalar.copy(sums[:], banks[aside][:])
+                done = sb("done_aside", [P, 2, CHUNK], F32)
+                nc.gpsimd.tensor_tensor(done[:], sums[:], res_t[aside][:], ALU.add)
+                store(aside[0], aside[1], done)
             for pair in range(2):
                 acc = psum.tile([P, 2, CHUNK], F32, name="o_ps%d_%d" % (c, pair), tag="bank%d" % (2 * c + pair))
+                banks[c, pair] = acc
                 for i in range(2):
                     cols = slice((2 * pair + i) * P, (2 * pair + i + 1) * P)
                     nc.tensor.matmul_mx(
                         out=acc[:, i, :], lhsT=w2_code[:, cols].bitcast(FP8X4), lhsT_scale=w2_scale[:, cols],
                         rhs=z2_code[:].bitcast(FP8X4), rhs_scale=z2_scale[:], start=True, stop=True,
                     )
-                done = sb("done%d_%d" % (c, pair), [P, 2, CHUNK], F32)
-                nc.vector.tensor_tensor(done[:], acc[:], res_t[c][:, 2 * pair : 2 * pair + 2, :], ALU.add)
-                nc.sync.dma_start(out_rows[:, 2 * pair : 2 * pair + 2, slots], done[:])
+                if (c, pair) != aside:
+                    done = sb("done%d_%d" % (c, pair), [P, 2, CHUNK], F32)
+                    nc.vector.tensor_tensor(done[:], acc[:], res_t[c, pair][:], ALU.add)
+                    store(c, pair, done)

from contextlib import ExitStack

import concourse.mybir as mybir

K, T, S, N, H, G, U = 512, 1024, 512, 512, 512, 2048, 1024
FLOPS = 2 * K * H * S + 2 * K * H * S + 2 * H * N * U

F32 = mybir.dt.float32
BF16 = mybir.dt.bfloat16
I32 = mybir.dt.int32
U32 = mybir.dt.uint32
U16 = mybir.dt.uint16
U8 = mybir.dt.uint8
FP8X4 = mybir.dt.float8_e4m3fn_x4
ALU = mybir.AluOpType
ACT = mybir.ActivationFunctionType

P = 128
PACK = 4
CHUNK = 256


def tile_picked_pqktrackpagex_none_p_kernel(
    tc, x_words, x_scales, w1, gs, d_words, d_scales, mem, res, gn, w2, offs, n1, n2, kidx, n3, out
):
    nc = tc.nc
    with ExitStack() as ctx:
        lists = ctx.enter_context(tc.tile_pool(name="lists", bufs=1))
        keep = ctx.enter_context(tc.tile_pool(name="keep", bufs=1))
        psum = ctx.enter_context(tc.psum_pool(name="psum", bufs=1))

        def sb(name, shape, dtype, over=None):
            return keep.tile(shape, dtype, name=name, tag=over or name, align_bytes=64)

        def load_list(name, src):
            tl = lists.tile([P, S // 16], U16, name=name)
            nc.sync.dma_start(tl[:], src)
            return tl

        xs_win = sb("xs_win", [P, T], U8)
        ds_win = sb("ds_win", [P, G], U8)
        d_scale = sb("d_scale", [P, H], U8)
        y_win = [sb("y_win%d" % t, [P, 2 * S], F32) for t in range(PACK)]
        warm = sb("warm", [P, 16], F32)
        nc.gpsimd.memset(xs_win[:].bitcast(I32), 0)
        nc.vector.memset(ds_win[:].bitcast(I32), 0)
        nc.vector.memset(d_scale[:].bitcast(I32), 0)
        for t in range(PACK):
            nc.vector.memset(y_win[t][:, S:], 0.0)
        nc.scalar.activation(warm[:, 0:1], y_win[0][:, S : S + 1], ACT.Sigmoid)

        offs_t = load_list("offs_t", offs)
        xw_win = sb("xw_win", [P, T], I32)
        nc.sync.dma_start(xw_win[:], x_words[0].rearrange("p c r -> p (c r)").bitcast(I32))
        for q in range(4):
            nc.sync.dma_start(xs_win[32 * q : 32 * q + 4, :].bitcast(I32), x_scales[0, 4 * q : 4 * q + 4, :].bitcast(I32))
        kidx_t = load_list("kidx_t", kidx)
        dw_win = sb("dw_win", [P, G], I32)
        nc.sync.dma_start(dw_win[:], d_words[0].rearrange("p c r -> p (c r)").bitcast(I32))
        nc.sync.dma_start(ds_win[0:P:8, :].bitcast(I32), d_scales[0].bitcast(I32))
        w1_raw = sb("w1_raw", [P, PACK, H], F32)
        nc.sync.dma_start(w1_raw[:], w1.rearrange("(p j) c -> p j c", j=PACK))
        n3_t = load_list("n3_t", n3)
        page = [sb("page%d" % t, [P, U], F32) for t in range(PACK)]
        mem_rows = mem.rearrange("(a t b) u -> t a b u", t=PACK, b=8)
        nc.sync.dma_start(page[0][:], mem_rows[0])
        n1_t = load_list("n1_t", n1)
        n2_t = load_list("n2_t", n2)
        gs_t = sb("gs_t", [P, PACK], F32)
        nc.sync.dma_start(gs_t[:], gs.rearrange("(p t) o -> p (t o)", t=PACK))
        for t in range(1, PACK):
            nc.sync.dma_start(page[t][:], mem_rows[t])
        w2_raw = sb("w2_raw", [P, PACK, N], F32)
        w2_rows = w2.rearrange("(a t b) n -> t a b n", t=PACK, b=8)
        for t in range(PACK):
            nc.sync.dma_start(w2_raw[:, t, :], w2_rows[t])
        gn_t = [sb("gn_t%d" % t, [P, 1], F32) for t in range(PACK)]
        with nc.allow_non_contiguous_dma(reason="512 row factors, one value a row"):
            for t in range(PACK):
                nc.sync.dma_start(gn_t[t][:], gn.rearrange("(a t b) o -> t a b o", t=PACK, b=8)[t])
        chunks = U // CHUNK
        res_rows = res.rearrange("(m p) u -> p m u", p=P)
        res_t = {}
        for c in range(chunks):
            for pair in range(2):
                part = sb("res%d_%d" % (c, pair), [P, 2, CHUNK], F32)
                nc.sync.dma_start(part[:], res_rows[:, 2 * pair : 2 * pair + 2, c * CHUNK : (c + 1) * CHUNK])
                res_t[c, pair] = part

        x_code = sb("x_code", [P, S], U32)
        x_scale = sb("x_scale", [P, S], U8)
        nc.vector.tensor_copy(x_code[:], xw_win[:].bitcast(U32).indirect(offs_t[:]))
        nc.vector.tensor_copy(x_scale[:], xs_win[:].indirect(offs_t[:]))

        held = []

        def fetch_held(over):
            t = len(held)
            old = sb("held%d" % t, [P, S], F32, over=over)
            nc.vector.tensor_scalar(old[:], page[t][:].indirect(n3_t[:]), 0.5, 0.0, ALU.mult, ALU.add)
            held.append(old)

        d_pick = sb("d_pick", [P, H], U32)
        ds_pick = sb("ds_pick", [P, H], U8)
        nc.vector.tensor_copy(d_pick[:], dw_win[:].bitcast(U32).indirect(kidx_t[:]))
        nc.vector.tensor_copy(ds_pick[:], ds_win[:].indirect(kidx_t[:]))

        w1_bf = sb("w1_bf", [P, H * PACK], BF16)
        w1_dst = w1_bf[:].rearrange("p (t m j) -> p m j t", t=PACK, j=PACK)
        half = 72
        w1_src = w1_raw[:].rearrange("p j (m t) -> p m j t", t=PACK)
        nc.scalar.copy(w1_dst[:, 0:half], w1_src[:, 0:half])
        nc.vector.tensor_copy(w1_dst[:, half:P], w1_src[:, half:P])
        w1_code = sb("w1_code", [P, H], U32)
        w1_scale = sb("w1_scale", [P, H], U8)
        for h in range(2):
            cols = slice(h * (H // 2), (h + 1) * (H // 2))
            nc.vector.quantize_mx(
                out=w1_code[:, cols].bitcast(FP8X4),
                scales=w1_scale[:, cols],
                in_=w1_bf[:, h * 2 * H : (h + 1) * 2 * H],
            )
        y_ps = []
        for t in range(PACK):
            acc = psum.tile([P, S], F32, name="y_ps%d" % t, tag="bank%d" % t)
            cols = slice(t * P, (t + 1) * P)
            nc.tensor.matmul_mx(
                out=acc[:], lhsT=w1_code[:, cols].bitcast(FP8X4), lhsT_scale=w1_scale[:, cols],
                rhs=x_code[:].bitcast(FP8X4), rhs_scale=x_scale[:], start=True, stop=True,
            )
            y_ps.append(acc)

        d_code = sb("d_code", [P, H], U32, over="w1_bf")
        ds_dealt = sb("ds_dealt", [P, H], U8, over="w1_raw")
        nc.vector.tensor_copy(
            d_code[:].rearrange("p (t a b) -> p a t b", t=PACK, b=8),
            d_pick[:].rearrange("p (a t b) -> p a t b", t=PACK, b=8),
        )
        nc.vector.tensor_copy(
            ds_dealt[:].bitcast(I32).rearrange("p (t a b) -> p t a b", t=PACK, b=2),
            ds_pick[:].bitcast(I32).rearrange("p (a t b) -> p t a b", t=PACK, b=2),
        )
        for r in range(4):
            nc.sync.dma_start(d_scale[r:P:32, :].bitcast(I32), ds_dealt[8 * r : P : 32, :].bitcast(I32))

        for t in range(PACK - 1):
            fetch_held(None)

        near = sb("near", [P, PACK, S], F32)
        stay = sb("stay", [P, PACK, S], F32)
        for t in range(PACK):
            nc.scalar.copy(y_win[t][:, 0:S], y_ps[t][:])
            sig = sb("sig%d" % t, [P, S], F32)
            nc.scalar.activation(sig[:], y_win[t][:].indirect(n1_t[:]), ACT.Sigmoid)
            gate = sb("gate%d" % t, [P, S], F32)
            nc.gpsimd.tensor_scalar(gate[:], sig[:], gs_t[:, t : t + 1], 0.0, ALU.mult, ALU.add)
            other = sb("other%d" % t, [P, S], F32)
            nc.vector.tensor_copy(other[:], y_win[t][:].indirect(n2_t[:]))
            nc.gpsimd.tensor_tensor(near[:, t, :], other[:], gate[:], ALU.mult)
            nc.vector.scalar_tensor_tensor(
                stay[:, t, :], gate[:], gs_t[:, t : t + 1], y_ps[t][:], ALU.subtract, ALU.mult
            )
        z_bf = sb("z_bf", [P, S * PACK], BF16)
        z_dst = z_bf[:].rearrange("p (c i t) -> p c t i", i=2, t=PACK)
        for h in range(2):
            pairs = slice(h * (S // 4), (h + 1) * (S // 4))
            nc.vector.tensor_tensor(
                z_dst[:, pairs],
                near[:].rearrange("p t (c i) -> p c t i", i=2)[:, pairs],
                stay[:].rearrange("p t (c i) -> p c t i", i=2)[:, pairs],
                ALU.subtract,
            )

        w2_bf = sb("w2_bf", [P, N * PACK], BF16, over="sig3")
        nc.scalar.copy(
            w2_bf[:].rearrange("p (c i t) -> p c t i", i=4, t=PACK),
            w2_raw[:].rearrange("p t (c i) -> p c t i", i=4),
        )
        z_code = sb("z_code", [P, S], U32)
        z_scale = sb("z_scale", [P, S], U8)
        for h in range(2):
            cols = slice(h * (S // 2), (h + 1) * (S // 2))
            nc.vector.quantize_mx(
                out=z_code[:, cols].bitcast(FP8X4), scales=z_scale[:, cols], in_=z_bf[:, h * 2 * S : (h + 1) * 2 * S]
            )
        fetch_held("z_bf")

        scores = []
        for t in range(PACK):
            acc = psum.tile([P, S], F32, name="s_ps%d" % t, tag="bank%d" % (PACK + t))
            cols = slice(t * P, (t + 1) * P)
            nc.tensor.matmul_mx(
                out=acc[:], lhsT=d_code[:, cols].bitcast(FP8X4), lhsT_scale=d_scale[:, cols],
                rhs=z_code[:].bitcast(FP8X4), rhs_scale=z_scale[:], start=True, stop=True,
            )
            scores.append(acc)
        new = []
        for t in range(PACK):
            top = sb("new%d" % t, [P, S], F32)
            if t < 2:
                nc.vector.scalar_tensor_tensor(top[:], scores[t][:], 0.0625, held[t][:], ALU.mult, ALU.max)
            else:
                score = sb("score%d" % t, [P, S], F32)
                nc.scalar.activation(score[:], scores[t][:], ACT.Copy, scale=0.0625)
                gap = sb("gap%d" % t, [P, S], F32)
                nc.gpsimd.tensor_tensor(gap[:], score[:], held[t][:], ALU.subtract)
                nc.scalar.activation(top[:], gap[:], ACT.Relu)
            new.append(top)
        z2_bf = sb("z2_bf", [P, U, PACK], BF16, over="gap3")
        for t in range(PACK):
            if t < 2:
                nc.vector.tensor_copy(page[t][:].indirect(n3_t[:]), new[t][:])
            else:
                nc.vector.tensor_tensor(page[t][:].indirect(n3_t[:]), held[t][:], new[t][:], ALU.add)
            width = CHUNK if t == PACK - 1 else U
            for c0 in range(0, U, width):
                nc.scalar.activation(
                    z2_bf[:, c0 : c0 + width, t], page[t][:, c0 : c0 + width], ACT.Copy, scale=gn_t[t][:]
                )

        w2_code = sb("w2_code", [P, N], U32, over="new2")
        w2_scale = sb("w2_scale", [P, N], U8)
        nc.vector.quantize_mx(out=w2_code[:].bitcast(FP8X4), scales=w2_scale[:], in_=w2_bf[:])

        out_rows = out.rearrange("(m p) u -> p m u", p=P)

        def store(c, pair, done):
            nc.sync.dma_start(out_rows[:, 2 * pair : 2 * pair + 2, c * CHUNK : (c + 1) * CHUNK], done[:])

        aside = (1, 1)
        banks = {}
        for c in range(chunks):
            slots = slice(c * CHUNK, (c + 1) * CHUNK)
            z2_code = sb("z2_code%d" % c, [P, CHUNK], U32, over="res0_%d" % (c - 2) if c >= 2 else None)
            z2_scale = sb("z2_scale%d" % c, [P, CHUNK], U8)
            nc.vector.quantize_mx(
                out=z2_code[:].bitcast(FP8X4), scales=z2_scale[:], in_=z2_bf[:, slots, :].rearrange("p c t -> p (c t)")
            )
            if c == chunks - 1:
                sums = sb("sums", [P, 2, CHUNK], F32, over="gap3")
                nc.scalar.copy(sums[:], banks[aside][:])
                done = sb("done_aside", [P, 2, CHUNK], F32)
                nc.gpsimd.tensor_tensor(done[:], sums[:], res_t[aside][:], ALU.add)
                store(aside[0], aside[1], done)
            for pair in range(2):
                acc = psum.tile([P, 2, CHUNK], F32, name="o_ps%d_%d" % (c, pair), tag="bank%d" % (2 * c + pair))
                banks[c, pair] = acc
                for i in range(2):
                    cols = slice((2 * pair + i) * P, (2 * pair + i + 1) * P)
                    nc.tensor.matmul_mx(
                        out=acc[:, i, :], lhsT=w2_code[:, cols].bitcast(FP8X4), lhsT_scale=w2_scale[:, cols],
                        rhs=z2_code[:].bitcast(FP8X4), rhs_scale=z2_scale[:], start=True, stop=True,
                    )
                if (c, pair) != aside:
                    done = sb("done%d_%d" % (c, pair), [P, 2, CHUNK], F32)
                    nc.vector.tensor_tensor(done[:], acc[:], res_t[c, pair][:], ALU.add)
                    store(c, pair, done)
